import numpy as np
import ml_dtypes


def mxq(x, axis, fmt="e4m3"):
    dtype, down = {"e4m3": (ml_dtypes.float8_e4m3fn, 7), "e5m2": (ml_dtypes.float8_e5m2, 14)}[fmt]
    v = np.moveaxis(np.asarray(x, np.float32).astype(ml_dtypes.bfloat16).astype(np.float64), axis, -1)
    blocks = v.reshape(v.shape[:-1] + (-1, 32))
    amax = np.abs(blocks).max(-1, keepdims=True)
    byte = np.maximum(np.where(amax > 0, np.frexp(amax)[1] - 1 + 127, 0) - down, 1)
    scale = np.exp2(byte - 127.0)
    codes = (blocks / scale).astype(np.float32).astype(dtype).astype(np.float64)
    return np.moveaxis((codes * scale).reshape(v.shape), -1, axis)


WIDE = False


def mx_kscale(k):
    if not WIDE:
        return np.ones(k)
    levels = np.array([10, -10, 5, -5, 0])
    if k % 512:
        return np.exp2(np.random.permutation(np.resize(levels, k // 32))).repeat(32)
    a = np.empty((k // 512, 16))
    for p in range(k // 512):
        a[p, :8] = np.random.permutation(np.resize(levels, 8))
        for g in range(8):
            far = levels[np.abs(levels - a[p, g]) >= 10]
            a[p, g + 8] = far[np.random.randint(len(far))]
    return np.exp2(a.ravel()).repeat(32)


def f64(x):
    return np.asarray(x).astype(np.float64)


def striped(idx):
    return np.tile(idx.reshape(-1, 16).T, (8, 1)).astype(np.uint16)


def unstriped(offs):
    return offs[:16].T.reshape(-1).astype(np.int64)


E2M1 = np.array([0.0, 0.5, 1.0, 1.5, 2.0, 3.0, 4.0, 6.0, -0.0, -0.5, -1.0, -1.5, -2.0, -3.0, -4.0, -6.0])


def pack_weight(w, fmt):
    k, n = w.shape
    w = f64(np.asarray(w, np.float32).astype(ml_dtypes.bfloat16)).reshape(k // 32, 32, n)
    amax = np.abs(w).max(1)
    if fmt == "e4m3":
        byte = np.frexp(amax)[1] - 1 + 127 - 7
    else:
        mant, ex = np.frexp(amax / 6.0)
        byte = np.where(mant > 0.5, ex, ex - 1) + 127
    byte = np.clip(np.where(amax > 0, byte, 1), 1, 254)
    scaled = (w * np.exp2(127.0 - byte)[:, None, :]).reshape(k, n).astype(np.float32)
    by_word = np.ascontiguousarray(scaled.reshape(k // 512, 128, 4, n).transpose(0, 1, 3, 2))
    if fmt == "e4m3":
        words = by_word.astype(ml_dtypes.float8_e4m3fn).view(np.uint8)
    else:
        c = by_word.astype(ml_dtypes.float4_e2m1fn).view(np.uint8) & 0xF
        words = (c[..., 0::2] | (c[..., 1::2] << 4)).reshape(k // 512, 128, 2 * n)
    return np.ascontiguousarray(words), np.ascontiguousarray(byte.astype(np.uint8).reshape(k // 512, 16, n))


def unpack_weight(words, scales, fmt):
    g, _, n = scales.shape
    words = np.ascontiguousarray(words).reshape(g, 128, n, -1)
    if fmt == "e4m3":
        vals = words.view(ml_dtypes.float8_e4m3fn).astype(np.float64)
    else:
        nib = np.empty((g, 128, n, 4), np.uint8)
        nib[..., 0::2] = words & 0xF
        nib[..., 1::2] = words >> 4
        vals = E2M1[nib]
    vals = vals * np.repeat(np.exp2(scales.astype(np.float64) - 127.0), 8, axis=1)[..., None]
    return vals.transpose(0, 1, 3, 2).reshape(g * 512, n)


def sigmoid(v):
    return 1.0 / (1.0 + np.exp(-np.maximum(v, -700.0)))


K, T, Q, E, C, D, H = 512, 768, 512, 6, 128, 256, 512
N = 256


def by_expert(wq, xq, C):
    return np.concatenate([wq[e].T @ xq[:, e * C:(e + 1) * C] for e in range(E)], axis=1)


def setup_inputs():
    n = np.random.standard_normal
    s = mx_kscale(K)
    u = mx_kscale(H)
    slot_token = np.random.permutation(T)[:E * C]
    slots2 = np.concatenate([np.random.permutation(Q)[:D] for e in range(E)])
    x = pack_weight(n((K, Q)) * s[:, None], "e4m3")
    w1 = [pack_weight(m, "e2m1") for m in n((E, K, H)) / np.sqrt(K) / s[None, :, None]]
    w3 = [pack_weight(m, "e2m1") for m in n((E, K, H)) / np.sqrt(K) / s[None, :, None] * u]
    w2 = [pack_weight(m, "e2m1") for m in n((E, H, N)) / np.sqrt(H) / u[None, :, None]]
    return {
        "x_words": x[0],
        "x_scales": x[1],
        "xo": (n((K, T)) * s[:, None]).astype(np.float32),
        "w1_words": np.stack([m[0] for m in w1]),
        "w1_scales": np.stack([m[1] for m in w1]),
        "w3_words": np.stack([m[0] for m in w3]),
        "w3_scales": np.stack([m[1] for m in w3]),
        "w2_words": np.stack([m[0] for m in w2]),
        "w2_scales": np.stack([m[1] for m in w2]),
        "gate": np.tile(np.random.uniform(0.2, 1.0, E * C), (128, 1)).astype(np.float32),
        "offs": striped(slot_token),
        "offs2": striped(slots2),
    }


def reference(x_words, x_scales, xo, w1_words, w1_scales, w3_words, w3_scales, w2_words, w2_scales, gate, offs, offs2):
    w1 = np.stack([unpack_weight(w1_words[e], w1_scales[e], "e2m1") for e in range(E)])
    w3 = np.stack([unpack_weight(w3_words[e], w3_scales[e], "e2m1") for e in range(E)])
    w2 = np.stack([unpack_weight(w2_words[e], w2_scales[e], "e2m1") for e in range(E)])
    idx, idx2 = unstriped(offs), unstriped(offs2)
    xq = mxq(f64(xo)[:, idx], 0, "e4m3")
    rq = unpack_weight(x_words, x_scales, "e4m3")[:, idx2]
    h = sigmoid(by_expert(w1, xq, C)) * by_expert(w3, xq, C)
    y = by_expert(w2, mxq(h, 0, "e4m3"), C)
    h = sigmoid(by_expert(w1, rq, D)) * by_expert(w3, rq, D)
    z = by_expert(w2, mxq(h, 0, "e4m3"), D)
    own = np.zeros((N, T))
    own[:, idx] = f64(gate[:1]) * y
    return np.concatenate([own, z], axis=1)

@@ -1,0 +1,341 @@
+from contextlib import ExitStack
+
+import concourse.mybir as mybir
+from concourse.masks import make_identity
+
+K, T, Q, E, C, D, H, N = 512, 768, 512, 6, 128, 256, 512, 256
+FLOPS = 2 * E * (C + D) * (2 * K * H + H * N)
+
+F32 = mybir.dt.float32
+BF16 = mybir.dt.bfloat16
+I32 = mybir.dt.int32
+U32 = mybir.dt.uint32
+U16 = mybir.dt.uint16
+U8 = mybir.dt.uint8
+FP8X4 = mybir.dt.float8_e4m3fn_x4
+FP4X4 = mybir.dt.float4_e2m1fn_x4
+MULT = mybir.AluOpType.mult
+SIGMOID = mybir.ActivationFunctionType.Sigmoid
+
+P = 128
+UNIT = 256
+LIST = 16
+CAST_PIECES = 1
+CAST_ON = 'ss'
+FAR_W = 6
+FAR_B = 5
+OWN_B = 3
+STEPPED = False
+A_B = 2
+B_B = 3
+T_B = 1
+Y_B = 2
+ON_GPSIMD = []
+GATE_ON = 'fused'
+H_B = 5
+SIG_B = 3
+HT_B = 3
+PROGRAM = [
+    ('warm',),
+    ('zero', 'v', 'w2'),
+    ('ident',),
+    ('load', 'sp', 'xw'),
+    ('zero', 'v', 'w3'),
+    ('load', 'sp', 'far_list'),
+    ('load', 'g', 'w2', 0, 2),
+    ('load', 'sp', 'own_list'),
+    ('load', 'g', 'w1', 0, 2),
+    ('load', 'sp', 'xo', 1),
+    ('load', 'sp', 'xo', 0),
+    ('zero', 'v', 'xs'),
+    ('load', 'sp', 'w3s'),
+    ('load', 'g', 'w3', 0, 2),
+    ('load', 'sp', 'w2', 2, 6),
+    ('load', 'sp', 'w1', 4, 6),
+    ('load', 's', 'xs'),
+    ('load', 'sp', 'w3', 4, 6),
+    ('zero', 'v', 'w1'),
+    ('load', 'sp', 'w1', 2, 4),
+    ('load', 's', 'w1s'),
+    ('gw', 0),
+    ('cast', 0, 0),
+    ('gb', 0),
+    ('go', 1, 0),
+    ('hid', 'f', 0, 0),
+    ('go', 0, 0),
+    ('cast', 1, 0),
+    ('hid', 'f', 0, 1),
+    ('go', 1, 1),
+    ('go', 0, 1),
+    ('qo', 0),
+    ('load', 'sp', 'w2s'),
+    ('gw', 4),
+    ('hid', 'o', 0, 1),
+    ('turn', 'f', 0),
+    ('go', 2, 0),
+    ('go', 2, 1),
+    ('qo', 1),
+    ('hid', 'o', 0, 0),
+    ('qh', 'f', 0),
+    ('load', 'sp', 'gate'),
+    ('turn', 'o', 0),
+    ('qo', 2),
+    ('gw', 1),
+    ('load', 'g', 'w3', 2, 4),
+    ('qh', 'o', 0),
+    ('hid', 'o', 1, 0),
+    ('hid', 'o', 1, 1),
+    ('sf', 0),
+    ('turn', 'o', 1),
+    ('hid', 'o', 2, 0),
+    ('gb', 1),
+    ('hid', 'o', 2, 1),
+    ('turn', 'o', 2),
+    ('qh', 'o', 2),
+    ('gb', 2),
+    ('so', 0, 0),
+    ('hid', 'f', 1, 1),
+    ('gw', 2),
+    ('qh', 'o', 1),
+    ('hid', 'f', 2, 0),
+    ('hid', 'f', 1, 0),
+    ('hid', 'f', 2, 1),
+    ('sc', 0, 0),
+    ('so', 1, 0),
+    ('gw', 3),
+    ('turn', 'f', 1),
+    ('turn', 'f', 2),
+    ('gw', 5),
+    ('gb', 3),
+    ('qh', 'f', 2),
+    ('sc', 1, 0),
+    ('hid', 'f', 3, 1),
+    ('so', 0, 1),
+    ('gb', 5),
+    ('so', 2, 0),
+    ('hid', 'f', 3, 0),
+    ('gb', 4),
+    ('hid', 'f', 4, 0),
+    ('sc', 2, 0),
+    ('turn', 'f', 3),
+    ('so', 1, 1),
+    ('qh', 'f', 1),
+    ('hid', 'f', 5, 1),
+    ('sf', 1),
+    ('hid', 'f', 4, 1),
+    ('hid', 'f', 5, 0),
+    ('so', 2, 1),
+    ('sf', 2),
+    ('sc', 1, 1),
+    ('turn', 'f', 4),
+    ('turn', 'f', 5),
+    ('qh', 'f', 3),
+    ('sf', 3),
+    ('qh', 'f', 4),
+    ('qh', 'f', 5),
+    ('sc', 2, 1),
+    ('sf', 4),
+    ('sc', 0, 1),
+    ('sf', 5),
+]
+
+
+def tile_moe_loc_glu_sigmoid_kernel(tc, x_words, x_scales, xo, w1_words, w1_scales, w3_words, w3_scales, w2_words, w2_scales, gate, offs, offs2, out):
+    nc = tc.nc
+    with ExitStack() as ctx:
+        keep = ctx.enter_context(tc.tile_pool(name="keep", bufs=1))
+        psum = ctx.enter_context(tc.psum_pool(name="psum", bufs=1))
+        queue = {"sp": nc.sync, "s": nc.scalar, "g": nc.gpsimd}
+
+        own_list = keep.tile([P, E * C // LIST], U16, name="own_list")
+        far_list = keep.tile([P, E * D // LIST], U16, name="far_list")
+        xw = keep.tile([P, Q], I32, name="xw", align_bytes=64)
+        xs = keep.tile([P, Q], U8, name="xs", align_bytes=64)
+        words = {"w1": keep.tile([P, E, 2 * H], U8, name="w1w", align_bytes=64),
+                 "w3": keep.tile([P, E, 2 * H], U8, name="w3w", align_bytes=64),
+                 "w2": keep.tile([P, E, 2 * N], U8, name="w2w", align_bytes=64)}
+        planes = {"w1": keep.tile([P, E, H], U8, name="w1s", align_bytes=64),
+                  "w3": keep.tile([P, E, H], U8, name="w3s", align_bytes=64),
+                  "w2": keep.tile([P, E, N], U8, name="w2s", align_bytes=64)}
+        words_hbm = {"w1": w1_words, "w3": w3_words, "w2": w2_words}
+        planes_hbm = {"w1": w1_scales, "w3": w3_scales, "w2": w2_scales}
+        ident = keep.tile([P, P], F32, name="ident")
+        gate_sb = keep.tile([P, E * C], F32, name="gate_sb")
+        xo_raw = [keep.tile([P, 2, T], F32, name="xo_raw%d" % u) for u in range(2)]
+        xo_pair = [keep.tile([P, T, 2], BF16, name="xo_pair%d" % u) for u in range(2)]
+        own_out = [keep.tile([P, T], F32, name="own_out%d" % h) for h in range(2)]
+        xo_rows = xo.rearrange("(p u e) t -> u p e t", u=2, e=2)
+        state = {}
+        slots = {}
+        uses = {}
+
+        def fresh(pool, name, shape, dtype, count):
+            if name not in slots:
+                slots[name] = [pool.tile(shape, dtype, name="%s%d" % (name, i), align_bytes=64 if pool is keep else None) for i in range(count)]
+            uses[name] = uses.get(name, -1) + 1
+            return slots[name][uses[name] % count]
+
+        def load(q, what, a=0, b=0):
+            eng = queue[q]
+            if what == "far_list":
+                nc.sync.dma_start(far_list[:], offs2)
+            elif what == "own_list":
+                nc.sync.dma_start(own_list[:], offs)
+            elif what == "xw":
+                eng.dma_start(out=xw[:], in_=x_words[0].rearrange("p t d -> p (t d)").bitcast(I32))
+            elif what == "xs":
+                for r in range(4):
+                    eng.dma_start(out=xs[32 * r : 32 * r + 4, :].bitcast(I32), in_=x_scales[0, 4 * r : 4 * r + 4, :].bitcast(I32))
+            elif what == "xo":
+                eng.dma_start(out=xo_raw[a][:], in_=xo_rows[a])
+            elif what == "gate":
+                eng.dma_start(out=gate_sb[:], in_=gate)
+            elif what in words:
+                eng.dma_start(out=words[what][:, a:b, :].bitcast(I32), in_=words_hbm[what].rearrange("e s p b -> p (e s) b")[:, a:b, :].bitcast(I32))
+            else:
+                rows = planes_hbm[what[:2]].rearrange("e s (q r) i -> q r (e s) i", r=4)
+                for r in range(4):
+                    eng.dma_start(out=planes[what[:2]][32 * r : 32 * r + 4, :, :].bitcast(I32), in_=rows[r].bitcast(I32))
+
+        def experts(kind, j):
+            return (j, j) if kind == "f" else (2 * j, 2 * j + 1)
+
+        def list_cols(j):
+            return slice(j * UNIT // LIST, (j + 1) * UNIT // LIST)
+
+        def cast(u, c):
+            cols = slice(c * T // CAST_PIECES, (c + 1) * T // CAST_PIECES)
+            src = xo_raw[u][:, :, cols].rearrange("p e t -> p t e")
+            if CAST_ON[u] == "s":
+                nc.scalar.copy(out=xo_pair[u][:, cols, :], in_=src)
+            else:
+                nc.gpsimd.tensor_copy(out=xo_pair[u][:, cols, :], in_=src)
+
+        def gather_words(j):
+            codes = fresh(keep, "far_codes", [P, UNIT], U32, FAR_W)
+            nc.vector.tensor_copy(codes[:], xw[:].bitcast(U32).indirect(far_list[:, list_cols(j)]))
+            state["codes", "f", j] = codes
+
+        def gather_bytes(j):
+            scales = fresh(keep, "far_bytes", [P, UNIT], U8, FAR_B)
+            nc.vector.tensor_copy(scales[:], xs[:].indirect(far_list[:, list_cols(j)]))
+            state["scales", "f", j] = scales
+
+        def gather_own(j, u):
+            window = xo_pair[u][:].rearrange("p t e -> p (t e)").bitcast(U32)
+            if u == 0:
+                state["picked", j] = fresh(keep, "picked", [P, 4 * UNIT], BF16, OWN_B)
+            if STEPPED:
+                dst = state["picked", j][:].bitcast(U32).rearrange("p (s u) -> p s u", u=2)[:, :, u]
+            else:
+                if u == 0:
+                    state["pairs", j] = fresh(keep, "pairs", [P, 2, 2 * UNIT], BF16, OWN_B)
+                dst = state["pairs", j][:, u, :].bitcast(U32)
+            nc.vector.tensor_copy(dst, window.indirect(own_list[:, list_cols(j)]))
+
+        def quant_own(j):
+            picked = state["picked", j]
+            if not STEPPED:
+                nc.scalar.copy(out=picked[:].bitcast(F32).rearrange("p (s u) -> p s u", u=2),
+                               in_=state["pairs", j][:].bitcast(F32).rearrange("p u s -> p s u"))
+            codes = keep.tile([P, UNIT], U32, name="own_codes%d" % j, align_bytes=64)
+            scales = keep.tile([P, UNIT], U8, name="own_bytes%d" % j, align_bytes=64)
+            nc.vector.quantize_mx(out=codes[:].bitcast(FP8X4), scales=scales[:], in_=picked[:])
+            state["codes", "o", j] = codes
+            state["scales", "o", j] = scales
+
+        def hidden(kind, j, st):
+            codes, scales = state["codes", kind, j], state["scales", kind, j]
+            e = experts(kind, j)[st]
+            sl = slice(st * P, (st + 1) * P)
+            a = fresh(psum, "a", [P, H], F32, A_B)
+            b = fresh(psum, "b", [P, H], F32, B_B)
+            for acc, w in ((a, "w1"), (b, "w3")):
+                nc.tensor.matmul_mx(out=acc[:], lhsT=codes[:, sl].bitcast(FP8X4), lhsT_scale=scales[:, sl],
+                                    rhs=words[w][:, e, :].bitcast(FP4X4), rhs_scale=planes[w][:, e, :], start=True, stop=True)
+            sig = fresh(keep, "sig", [P, 2, P, 2], F32, SIG_B)
+            nc.scalar.activation(out=sig[:], in_=a[:].rearrange("s (q u e) -> s u q e", u=2, e=2), func=SIGMOID)
+            h = fresh(keep, "h", [P, H], BF16, H_B)
+            state["h", kind, j, st] = h
+            if (kind, j, st) in ON_GPSIMD:
+                b_sb = fresh(keep, "b_sb", [P, 2, P, 2], F32, 4)
+                nc.scalar.copy(out=b_sb[:], in_=b[:].rearrange("s (q u e) -> s u q e", u=2, e=2))
+                nc.gpsimd.tensor_tensor(out=h[:], in0=b_sb[:].rearrange("s u q e -> s (u q e)"), in1=sig[:].rearrange("s u q e -> s (u q e)"), op=MULT)
+            else:
+                nc.vector.tensor_tensor(out=h[:].rearrange("s (u q e) -> s u q e", u=2, e=2),
+                                        in0=b[:].rearrange("s (q u e) -> s u q e", u=2, e=2), in1=sig[:], op=MULT)
+
+        def turn(kind, j):
+            turned = fresh(psum, "turned", [P, 2, 2, P], F32, T_B)
+            for st in range(2):
+                for u in range(2):
+                    nc.tensor.transpose(turned[:, st, u, :], state["h", kind, j, st][:].bitcast(F32)[:, u * P : (u + 1) * P], ident[:])
+            ht = fresh(keep, "ht", [P, 4 * UNIT], BF16, HT_B)
+            nc.scalar.copy(out=ht[:].bitcast(F32).rearrange("p (t s u) -> p t s u", t=2, u=2), in_=turned[:].rearrange("p t u s -> p t s u"))
+            state["ht", kind, j] = ht
+
+        def quant_h(kind, j):
+            codes = keep.tile([P, UNIT], U32, name="h_codes_%s%d" % (kind, j), align_bytes=64)
+            scales = keep.tile([P, UNIT], U8, name="h_bytes_%s%d" % (kind, j), align_bytes=64)
+            nc.vector.quantize_mx(out=codes[:].bitcast(FP8X4), scales=scales[:], in_=state["ht", kind, j][:])
+            state["hq", kind, j] = (codes, scales)
+
+        def product(dst, e, half, codes, scales):
+            nc.tensor.matmul_mx(out=dst, lhsT=words["w2"][:, e, half * 2 * P : (half + 1) * 2 * P].bitcast(FP4X4),
+                                lhsT_scale=planes["w2"][:, e, half * P : (half + 1) * P],
+                                rhs=codes.bitcast(FP8X4), rhs_scale=scales, start=True, stop=True)
+
+        def second_far(j):
+            codes, scales = state["hq", "f", j]
+            y = fresh(psum, "y", [P, 2, UNIT], F32, Y_B)
+            for half in range(2):
+                product(y[:, half, :], j, half, codes[:], scales[:])
+            res = fresh(keep, "res", [P, 2, UNIT], F32, 4)
+            nc.scalar.copy(out=res[:], in_=y[:])
+            nc.sync.dma_start(out=out.rearrange("(h p) c -> p h c", p=P)[:, :, T + j * D : T + (j + 1) * D], in_=res[:])
+
+        def second_own(j, half):
+            codes, scales = state["hq", "o", j]
+            y = fresh(psum, "y", [P, 2, UNIT], F32, Y_B)[:, 0, :]
+            for st in range(2):
+                sl = slice(st * P, (st + 1) * P)
+                product(y[:, sl], 2 * j + st, half, codes[:, sl], scales[:, sl])
+            res = fresh(keep, "res_own", [P, UNIT], F32, 6)
+            gates = gate_sb[:, j * UNIT : (j + 1) * UNIT]
+            if GATE_ON == "fused":
+                nc.scalar.copy(out=res[:], in_=y[:])
+            elif GATE_ON == "v":
+                nc.vector.tensor_tensor(out=res[:], in0=y[:], in1=gates, op=MULT)
+            else:
+                raw = fresh(keep, "raw_own", [P, UNIT], F32, 4)
+                nc.scalar.copy(out=raw[:], in_=y[:])
+                nc.gpsimd.tensor_tensor(out=res[:], in0=raw[:], in1=gates, op=MULT)
+            state["res", j, half] = res
+
+        def scatter(j, half):
+            res = state["res", j, half]
+            window = own_out[half][:].indirect(own_list[:, list_cols(j)])
+            if GATE_ON == "fused":
+                nc.vector.tensor_tensor(window, res[:], gate_sb[:, j * UNIT : (j + 1) * UNIT], MULT)
+            else:
+                nc.vector.tensor_copy(window, res[:])
+            state["scattered", half] = state.get(("scattered", half), 0) + 1
+            if state["scattered", half] == 3:
+                nc.sync.dma_start(out=out[half * P : (half + 1) * P, 0:T], in_=own_out[half][:])
+
+        def zero(eng, what):
+            plane = xs if what == "xs" else planes[what]
+            (nc.vector if eng == "v" else nc.gpsimd).memset(plane[:].bitcast(I32), 0)
+
+        def warm():
+            seed = keep.tile([P, 2], F32, name="seed")
+            nc.vector.memset(seed[:, 0:1], 0.0)
+            nc.scalar.activation(out=seed[:, 1:2], in_=seed[:, 0:1], func=SIGMOID)
+
+        def identity():
+            make_identity(nc, ident[:])
+
+        steps = {"load": load, "cast": cast, "gw": gather_words, "gb": gather_bytes, "go": gather_own, "qo": quant_own,
+                 "hid": hidden, "turn": turn, "qh": quant_h, "sf": second_far, "so": second_own, "sc": scatter, "zero": zero, "ident": identity, "warm": warm}
+        for step in PROGRAM:
+            steps[step[0]](*step[1:])

@@ -18,324 +18,254 @@ MULT = mybir.AluOpType.mult
 SIGMOID = mybir.ActivationFunctionType.Sigmoid
 
 P = 128
-UNIT = 256
-LIST = 16
-CAST_PIECES = 1
-CAST_ON = 'ss'
-FAR_W = 6
-FAR_B = 5
-OWN_B = 3
-STEPPED = False
-A_B = 2
-B_B = 3
-T_B = 1
-Y_B = 2
-ON_GPSIMD = []
-GATE_ON = 'fused'
-H_B = 5
-SIG_B = 3
-HT_B = 3
-PROGRAM = [
-    ('warm',),
-    ('zero', 'v', 'w2'),
-    ('ident',),
-    ('load', 'sp', 'xw'),
-    ('zero', 'v', 'w3'),
-    ('load', 'sp', 'far_list'),
-    ('load', 'g', 'w2', 0, 2),
-    ('load', 'sp', 'own_list'),
-    ('load', 'g', 'w1', 0, 2),
-    ('load', 'sp', 'xo', 1),
-    ('load', 'sp', 'xo', 0),
-    ('zero', 'v', 'xs'),
-    ('load', 'sp', 'w3s'),
-    ('load', 'g', 'w3', 0, 2),
-    ('load', 'sp', 'w2', 2, 6),
-    ('load', 'sp', 'w1', 4, 6),
-    ('load', 's', 'xs'),
-    ('load', 'sp', 'w3', 4, 6),
-    ('zero', 'v', 'w1'),
-    ('load', 'sp', 'w1', 2, 4),
-    ('load', 's', 'w1s'),
-    ('gw', 0),
-    ('cast', 0, 0),
-    ('gb', 0),
-    ('go', 1, 0),
-    ('hid', 'f', 0, 0),
-    ('go', 0, 0),
-    ('cast', 1, 0),
-    ('hid', 'f', 0, 1),
-    ('go', 1, 1),
-    ('go', 0, 1),
-    ('qo', 0),
-    ('load', 'sp', 'w2s'),
-    ('gw', 4),
-    ('hid', 'o', 0, 1),
-    ('turn', 'f', 0),
-    ('go', 2, 0),
-    ('go', 2, 1),
-    ('qo', 1),
-    ('hid', 'o', 0, 0),
-    ('qh', 'f', 0),
-    ('load', 'sp', 'gate'),
-    ('turn', 'o', 0),
-    ('qo', 2),
-    ('gw', 1),
-    ('load', 'g', 'w3', 2, 4),
-    ('qh', 'o', 0),
-    ('hid', 'o', 1, 0),
-    ('hid', 'o', 1, 1),
-    ('sf', 0),
-    ('turn', 'o', 1),
-    ('hid', 'o', 2, 0),
-    ('gb', 1),
-    ('hid', 'o', 2, 1),
-    ('turn', 'o', 2),
-    ('qh', 'o', 2),
-    ('gb', 2),
-    ('so', 0, 0),
-    ('hid', 'f', 1, 1),
-    ('gw', 2),
-    ('qh', 'o', 1),
-    ('hid', 'f', 2, 0),
-    ('hid', 'f', 1, 0),
-    ('hid', 'f', 2, 1),
-    ('sc', 0, 0),
-    ('so', 1, 0),
-    ('gw', 3),
-    ('turn', 'f', 1),
-    ('turn', 'f', 2),
-    ('gw', 5),
-    ('gb', 3),
-    ('qh', 'f', 2),
-    ('sc', 1, 0),
-    ('hid', 'f', 3, 1),
-    ('so', 0, 1),
-    ('gb', 5),
-    ('so', 2, 0),
-    ('hid', 'f', 3, 0),
-    ('gb', 4),
-    ('hid', 'f', 4, 0),
-    ('sc', 2, 0),
-    ('turn', 'f', 3),
-    ('so', 1, 1),
-    ('qh', 'f', 1),
-    ('hid', 'f', 5, 1),
-    ('sf', 1),
-    ('hid', 'f', 4, 1),
-    ('hid', 'f', 5, 0),
-    ('so', 2, 1),
-    ('sf', 2),
-    ('sc', 1, 1),
-    ('turn', 'f', 4),
-    ('turn', 'f', 5),
-    ('qh', 'f', 3),
-    ('sf', 3),
-    ('qh', 'f', 4),
-    ('qh', 'f', 5),
-    ('sc', 2, 1),
-    ('sf', 4),
-    ('sc', 0, 1),
-    ('sf', 5),
+GROUP = 256
+PER_COLUMN = 16
+FAR, OWN = "far", "own"
+SYNC, SCALAR = "sync", "scalar"
+
+W1_BANKS, W3_BANKS, TURN_BANKS, OUT_BANKS = 2, 3, 1, 2
+H_TILES = 9
+TURNED_TILES = 3
+
+REUSES_SIGMOID_TILE = {("scales", 3): (OWN, 0, 1), ("words", 3): (OWN, 1, 0), ("words", 4): (FAR, 1, 0)}
+
+STEPS = [
+    ("zero", "x"), ("zero", "w2"), ("load_far_list",), ("load_x_words", SYNC), ("zero", "w1"), ("load_x_scales", SYNC, 2, 4),
+    ("load_xo", SYNC, 0), ("load_x_scales", SCALAR, 0, 2), ("load_xo", SYNC, 1), ("load_own_list",),
+    ("load_words", SYNC, "w1", 0, 2), ("load_scales", SYNC, "w1", 2, 4, 0, 2), ("gather_scales", 0), ("round_xo", 1),
+    ("load_scales", SCALAR, "w1", 0, 2, 0, 6), ("zero", "w3"), ("round_xo", 0), ("gather_words", 2), ("gather_own", 0, 0),
+    ("load_words", SYNC, "w3", 0, 2), ("load_words", SYNC, "w1", 2, 4), ("identity",), ("load_sigmoid_table",),
+    ("load_scales", SCALAR, "w3", 2, 4, 0, 2), ("load_scales", SCALAR, "w3", 0, 2, 0, 6), ("gather_scales", 1),
+    ("gather_own", 2, 0), ("gather_scales", 2), ("gather_own", 1, 0), ("load_words", SYNC, "w2", 0, 2), ("gather_words", 0),
+    ("gather_own", 1, 1), ("load_words", SYNC, "w1", 4, 6), ("gather_words", 1), ("gather_own", 0, 1), ("hidden", FAR, 1, 1),
+    ("load_scales", SCALAR, "w1", 2, 4, 2, 6), ("hidden", FAR, 0, 0), ("quantize_own", 0), ("load_words", SYNC, "w3", 2, 4),
+    ("gather_own", 2, 1), ("quantize_own", 1), ("hidden", FAR, 1, 0), ("hidden", FAR, 0, 1), ("hidden", OWN, 0, 0),
+    ("gather_words", 4), ("load_scales", SYNC, "w3", 2, 4, 2, 6), ("hidden", OWN, 0, 1), ("turn", FAR, 1), ("turn", OWN, 0),
+    ("load_gate", SYNC), ("quantize_own", 2), ("hidden", OWN, 1, 0), ("load_words", SYNC, "w3", 4, 6),
+    ("load_scales", SYNC, "w2", 0, 2, 0, 6), ("load_scales", SYNC, "w2", 2, 4, 0, 6), ("quantize_hidden", FAR, 1),
+    ("turn", FAR, 0), ("gather_words", 5), ("quantize_hidden", OWN, 0), ("hidden", OWN, 1, 1), ("hidden", FAR, 2, 1),
+    ("turn", OWN, 1), ("load_words", SYNC, "w2", 2, 6), ("second_own", 0, 0), ("quantize_hidden", FAR, 0),
+    ("gather_words", 3), ("quantize_hidden", OWN, 1), ("hidden", OWN, 2, 0), ("hidden", OWN, 2, 1), ("gather_scales", 3),
+    ("hidden", FAR, 2, 0), ("scatter", 0, 0), ("gather_scales", 5), ("hidden", FAR, 5, 0), ("second_own", 0, 1),
+    ("second_far", 0), ("gather_scales", 4), ("hidden", FAR, 3, 0), ("turn", OWN, 2), ("turn", FAR, 2),
+    ("hidden", FAR, 3, 1), ("second_own", 1, 0), ("quantize_hidden", OWN, 2), ("quantize_hidden", FAR, 2),
+    ("hidden", FAR, 5, 1), ("scatter", 1, 0), ("second_far", 1), ("hidden", FAR, 4, 0), ("hidden", FAR, 4, 1),
+    ("turn", FAR, 3), ("second_own", 1, 1), ("store_far", SYNC, 0), ("quantize_hidden", FAR, 3), ("turn", FAR, 4),
+    ("second_far", 2), ("turn", FAR, 5), ("quantize_hidden", FAR, 4), ("quantize_hidden", FAR, 5), ("second_own", 2, 0),
+    ("second_far", 3), ("scatter", 0, 1), ("scatter", 1, 1), ("second_own", 2, 1), ("store_far", SCALAR, 2),
+    ("second_far_half", 4, 1), ("scatter", 2, 0), ("second_far_half", 4, 0), ("second_far_half", 5, 0),
+    ("store_far", SYNC, 3), ("store_far_half", SYNC, 4, 1), ("store_far", SCALAR, 1), ("scatter", 2, 1),
+    ("store_far_half", SCALAR, 5, 0), ("store_far_half", SCALAR, 4, 0), ("store_own", SCALAR, 1), ("second_far_half", 5, 1),
+    ("store_own", SCALAR, 0), ("store_far_half", SYNC, 5, 1),
 ]
 
 
-def tile_moe_loc_glu_sigmoid_kernel(tc, x_words, x_scales, xo, w1_words, w1_scales, w3_words, w3_scales, w2_words, w2_scales, gate, offs, offs2, out):
+def tile_moe_loc_glu_sigmoid_kernel(
+    tc, x_words, x_scales, xo, w1_words, w1_scales, w3_words, w3_scales, w2_words, w2_scales, gate, offs, offs2, out
+):
     nc = tc.nc
     with ExitStack() as ctx:
         keep = ctx.enter_context(tc.tile_pool(name="keep", bufs=1))
         psum = ctx.enter_context(tc.psum_pool(name="psum", bufs=1))
-        queue = {"sp": nc.sync, "s": nc.scalar, "g": nc.gpsimd}
+        queue = {SYNC: nc.sync, SCALAR: nc.scalar}
 
-        own_list = keep.tile([P, E * C // LIST], U16, name="own_list")
-        far_list = keep.tile([P, E * D // LIST], U16, name="far_list")
-        xw = keep.tile([P, Q], I32, name="xw", align_bytes=64)
-        xs = keep.tile([P, Q], U8, name="xs", align_bytes=64)
-        words = {"w1": keep.tile([P, E, 2 * H], U8, name="w1w", align_bytes=64),
-                 "w3": keep.tile([P, E, 2 * H], U8, name="w3w", align_bytes=64),
-                 "w2": keep.tile([P, E, 2 * N], U8, name="w2w", align_bytes=64)}
-        planes = {"w1": keep.tile([P, E, H], U8, name="w1s", align_bytes=64),
-                  "w3": keep.tile([P, E, H], U8, name="w3s", align_bytes=64),
-                  "w2": keep.tile([P, E, N], U8, name="w2s", align_bytes=64)}
+        own_list = keep.tile([P, E * C // PER_COLUMN], U16, name="own_list")
+        far_list = keep.tile([P, E * D // PER_COLUMN], U16, name="far_list")
+        far_words = keep.tile([P, Q], I32, name="far_words", align_bytes=64)
+        far_plane = keep.tile([P, Q], U8, name="far_plane", align_bytes=64)
+        width = {"w1": H, "w3": H, "w2": N}
+        words = {w: keep.tile([P, E, 2 * width[w]], U8, name=w + "_words", align_bytes=64) for w in width}
+        planes = {w: keep.tile([P, E, width[w]], U8, name=w + "_plane", align_bytes=64) for w in width}
         words_hbm = {"w1": w1_words, "w3": w3_words, "w2": w2_words}
-        planes_hbm = {"w1": w1_scales, "w3": w3_scales, "w2": w2_scales}
+        scales_hbm = {"w1": w1_scales, "w3": w3_scales, "w2": w2_scales}
         ident = keep.tile([P, P], F32, name="ident")
         gate_sb = keep.tile([P, E * C], F32, name="gate_sb")
+        xo_rows = xo.rearrange("(p u v) t -> u p v t", u=2, v=2)
         xo_raw = [keep.tile([P, 2, T], F32, name="xo_raw%d" % u) for u in range(2)]
-        xo_pair = [keep.tile([P, T, 2], BF16, name="xo_pair%d" % u) for u in range(2)]
-        own_out = [keep.tile([P, T], F32, name="own_out%d" % h) for h in range(2)]
-        xo_rows = xo.rearrange("(p u e) t -> u p e t", u=2, e=2)
-        state = {}
-        slots = {}
+        xo_pairs = [keep.tile([P, T, 2], BF16, name="xo_pairs%d" % u) for u in range(2)]
+        own_out = [keep.tile([P, T], F32, name="own_out%d" % half) for half in range(2)]
+
+        def several(pool, name, shape, dtype, count, align):
+            return [pool.tile(shape, dtype, name="%s%d" % (name, i), align_bytes=align) for i in range(count)]
+
+        in_turn = {
+            "w1_sums": several(psum, "w1_sums", [P, H], F32, W1_BANKS, None),
+            "w3_sums": several(psum, "w3_sums", [P, H], F32, W3_BANKS, None),
+            "turn_bank": several(psum, "turn_bank", [P, 2, 2, P], F32, TURN_BANKS, None),
+            "out_bank": several(psum, "out_bank", [P, 2, GROUP], F32, OUT_BANKS, None),
+            "h": several(keep, "h", [P, H], BF16, H_TILES, 64),
+            "turned": several(keep, "turned", [P, 4 * GROUP], BF16, TURNED_TILES, 64),
+        }
         uses = {}
 
-        def fresh(pool, name, shape, dtype, count):
-            if name not in slots:
-                slots[name] = [pool.tile(shape, dtype, name="%s%d" % (name, i), align_bytes=64 if pool is keep else None) for i in range(count)]
+        def next_tile(name):
             uses[name] = uses.get(name, -1) + 1
-            return slots[name][uses[name] % count]
+            return in_turn[name][uses[name] % len(in_turn[name])]
 
-        def load(q, what, a=0, b=0):
-            eng = queue[q]
-            if what == "far_list":
-                nc.sync.dma_start(far_list[:], offs2)
-            elif what == "own_list":
-                nc.sync.dma_start(own_list[:], offs)
-            elif what == "xw":
-                eng.dma_start(out=xw[:], in_=x_words[0].rearrange("p t d -> p (t d)").bitcast(I32))
-            elif what == "xs":
-                for r in range(4):
-                    eng.dma_start(out=xs[32 * r : 32 * r + 4, :].bitcast(I32), in_=x_scales[0, 4 * r : 4 * r + 4, :].bitcast(I32))
-            elif what == "xo":
-                eng.dma_start(out=xo_raw[a][:], in_=xo_rows[a])
-            elif what == "gate":
-                eng.dma_start(out=gate_sb[:], in_=gate)
-            elif what in words:
-                eng.dma_start(out=words[what][:, a:b, :].bitcast(I32), in_=words_hbm[what].rearrange("e s p b -> p (e s) b")[:, a:b, :].bitcast(I32))
-            else:
-                rows = planes_hbm[what[:2]].rearrange("e s (q r) i -> q r (e s) i", r=4)
-                for r in range(4):
-                    eng.dma_start(out=planes[what[:2]][32 * r : 32 * r + 4, :, :].bitcast(I32), in_=rows[r].bitcast(I32))
+        made = {}
 
-        def experts(kind, j):
-            return (j, j) if kind == "f" else (2 * j, 2 * j + 1)
+        def list_columns(j):
+            return slice(j * GROUP // PER_COLUMN, (j + 1) * GROUP // PER_COLUMN)
 
-        def list_cols(j):
-            return slice(j * UNIT // LIST, (j + 1) * UNIT // LIST)
+        def sigmoid_tag(kind, j, part):
+            return "sigmoid_%s%d%d" % (kind, j, part)
 
-        def cast(u, c):
-            cols = slice(c * T // CAST_PIECES, (c + 1) * T // CAST_PIECES)
-            src = xo_raw[u][:, :, cols].rearrange("p e t -> p t e")
-            if CAST_ON[u] == "s":
-                nc.scalar.copy(out=xo_pair[u][:, cols, :], in_=src)
-            else:
-                nc.gpsimd.tensor_copy(out=xo_pair[u][:, cols, :], in_=src)
+        def zero(name):
+            plane = far_plane if name == "x" else planes[name]
+            nc.vector.memset(plane[:].bitcast(I32), 0)
 
-        def gather_words(j):
-            codes = fresh(keep, "far_codes", [P, UNIT], U32, FAR_W)
-            nc.vector.tensor_copy(codes[:], xw[:].bitcast(U32).indirect(far_list[:, list_cols(j)]))
-            state["codes", "f", j] = codes
+        def load_far_list():
+            nc.sync.dma_start(far_list[:], offs2)
 
-        def gather_bytes(j):
-            scales = fresh(keep, "far_bytes", [P, UNIT], U8, FAR_B)
-            nc.vector.tensor_copy(scales[:], xs[:].indirect(far_list[:, list_cols(j)]))
-            state["scales", "f", j] = scales
+        def load_own_list():
+            nc.sync.dma_start(own_list[:], offs)
 
-        def gather_own(j, u):
-            window = xo_pair[u][:].rearrange("p t e -> p (t e)").bitcast(U32)
-            if u == 0:
-                state["picked", j] = fresh(keep, "picked", [P, 4 * UNIT], BF16, OWN_B)
-            if STEPPED:
-                dst = state["picked", j][:].bitcast(U32).rearrange("p (s u) -> p s u", u=2)[:, :, u]
-            else:
-                if u == 0:
-                    state["pairs", j] = fresh(keep, "pairs", [P, 2, 2 * UNIT], BF16, OWN_B)
-                dst = state["pairs", j][:, u, :].bitcast(U32)
-            nc.vector.tensor_copy(dst, window.indirect(own_list[:, list_cols(j)]))
+        def load_x_words(on):
+            queue[on].dma_start(out=far_words[:], in_=x_words[0].rearrange("p t d -> p (t d)").bitcast(I32))
 
-        def quant_own(j):
-            picked = state["picked", j]
-            if not STEPPED:
-                nc.scalar.copy(out=picked[:].bitcast(F32).rearrange("p (s u) -> p s u", u=2),
-                               in_=state["pairs", j][:].bitcast(F32).rearrange("p u s -> p s u"))
-            codes = keep.tile([P, UNIT], U32, name="own_codes%d" % j, align_bytes=64)
-            scales = keep.tile([P, UNIT], U8, name="own_bytes%d" % j, align_bytes=64)
-            nc.vector.quantize_mx(out=codes[:].bitcast(FP8X4), scales=scales[:], in_=picked[:])
-            state["codes", "o", j] = codes
-            state["scales", "o", j] = scales
+        def load_x_scales(on, q0, q1):
+            for q in range(q0, q1):
+                queue[on].dma_start(out=far_plane[32 * q : 32 * q + 4, :].bitcast(I32),
+                                    in_=x_scales[0, 4 * q : 4 * q + 4, :].bitcast(I32))
 
-        def hidden(kind, j, st):
-            codes, scales = state["codes", kind, j], state["scales", kind, j]
-            e = experts(kind, j)[st]
-            sl = slice(st * P, (st + 1) * P)
-            a = fresh(psum, "a", [P, H], F32, A_B)
-            b = fresh(psum, "b", [P, H], F32, B_B)
-            for acc, w in ((a, "w1"), (b, "w3")):
-                nc.tensor.matmul_mx(out=acc[:], lhsT=codes[:, sl].bitcast(FP8X4), lhsT_scale=scales[:, sl],
-                                    rhs=words[w][:, e, :].bitcast(FP4X4), rhs_scale=planes[w][:, e, :], start=True, stop=True)
-            sig = fresh(keep, "sig", [P, 2, P, 2], F32, SIG_B)
-            nc.scalar.activation(out=sig[:], in_=a[:].rearrange("s (q u e) -> s u q e", u=2, e=2), func=SIGMOID)
-            h = fresh(keep, "h", [P, H], BF16, H_B)
-            state["h", kind, j, st] = h
-            if (kind, j, st) in ON_GPSIMD:
-                b_sb = fresh(keep, "b_sb", [P, 2, P, 2], F32, 4)
-                nc.scalar.copy(out=b_sb[:], in_=b[:].rearrange("s (q u e) -> s u q e", u=2, e=2))
-                nc.gpsimd.tensor_tensor(out=h[:], in0=b_sb[:].rearrange("s u q e -> s (u q e)"), in1=sig[:].rearrange("s u q e -> s (u q e)"), op=MULT)
-            else:
-                nc.vector.tensor_tensor(out=h[:].rearrange("s (u q e) -> s u q e", u=2, e=2),
-                                        in0=b[:].rearrange("s (q u e) -> s u q e", u=2, e=2), in1=sig[:], op=MULT)
+        def load_xo(on, u):
+            queue[on].dma_start(out=xo_raw[u][:], in_=xo_rows[u])
 
-        def turn(kind, j):
-            turned = fresh(psum, "turned", [P, 2, 2, P], F32, T_B)
-            for st in range(2):
-                for u in range(2):
-                    nc.tensor.transpose(turned[:, st, u, :], state["h", kind, j, st][:].bitcast(F32)[:, u * P : (u + 1) * P], ident[:])
-            ht = fresh(keep, "ht", [P, 4 * UNIT], BF16, HT_B)
-            nc.scalar.copy(out=ht[:].bitcast(F32).rearrange("p (t s u) -> p t s u", t=2, u=2), in_=turned[:].rearrange("p t u s -> p t s u"))
-            state["ht", kind, j] = ht
+        def load_gate(on):
+            queue[on].dma_start(out=gate_sb[:], in_=gate)
 
-        def quant_h(kind, j):
-            codes = keep.tile([P, UNIT], U32, name="h_codes_%s%d" % (kind, j), align_bytes=64)
-            scales = keep.tile([P, UNIT], U8, name="h_bytes_%s%d" % (kind, j), align_bytes=64)
-            nc.vector.quantize_mx(out=codes[:].bitcast(FP8X4), scales=scales[:], in_=state["ht", kind, j][:])
-            state["hq", kind, j] = (codes, scales)
+        def load_words(on, w, e0, e1):
+            queue[on].dma_start(out=words[w][:, e0:e1, :].bitcast(I32),
+                                in_=words_hbm[w].rearrange("e s p b -> p (e s) b")[:, e0:e1, :].bitcast(I32))
 
-        def product(dst, e, half, codes, scales):
-            nc.tensor.matmul_mx(out=dst, lhsT=words["w2"][:, e, half * 2 * P : (half + 1) * 2 * P].bitcast(FP4X4),
-                                lhsT_scale=planes["w2"][:, e, half * P : (half + 1) * P],
-                                rhs=codes.bitcast(FP8X4), rhs_scale=scales, start=True, stop=True)
-
-        def second_far(j):
-            codes, scales = state["hq", "f", j]
-            y = fresh(psum, "y", [P, 2, UNIT], F32, Y_B)
-            for half in range(2):
-                product(y[:, half, :], j, half, codes[:], scales[:])
-            res = fresh(keep, "res", [P, 2, UNIT], F32, 4)
-            nc.scalar.copy(out=res[:], in_=y[:])
-            nc.sync.dma_start(out=out.rearrange("(h p) c -> p h c", p=P)[:, :, T + j * D : T + (j + 1) * D], in_=res[:])
-
-        def second_own(j, half):
-            codes, scales = state["hq", "o", j]
-            y = fresh(psum, "y", [P, 2, UNIT], F32, Y_B)[:, 0, :]
-            for st in range(2):
-                sl = slice(st * P, (st + 1) * P)
-                product(y[:, sl], 2 * j + st, half, codes[:, sl], scales[:, sl])
-            res = fresh(keep, "res_own", [P, UNIT], F32, 6)
-            gates = gate_sb[:, j * UNIT : (j + 1) * UNIT]
-            if GATE_ON == "fused":
-                nc.scalar.copy(out=res[:], in_=y[:])
-            elif GATE_ON == "v":
-                nc.vector.tensor_tensor(out=res[:], in0=y[:], in1=gates, op=MULT)
-            else:
-                raw = fresh(keep, "raw_own", [P, UNIT], F32, 4)
-                nc.scalar.copy(out=raw[:], in_=y[:])
-                nc.gpsimd.tensor_tensor(out=res[:], in0=raw[:], in1=gates, op=MULT)
-            state["res", j, half] = res
-
-        def scatter(j, half):
-            res = state["res", j, half]
-            window = own_out[half][:].indirect(own_list[:, list_cols(j)])
-            if GATE_ON == "fused":
-                nc.vector.tensor_tensor(window, res[:], gate_sb[:, j * UNIT : (j + 1) * UNIT], MULT)
-            else:
-                nc.vector.tensor_copy(window, res[:])
-            state["scattered", half] = state.get(("scattered", half), 0) + 1
-            if state["scattered", half] == 3:
-                nc.sync.dma_start(out=out[half * P : (half + 1) * P, 0:T], in_=own_out[half][:])
-
-        def zero(eng, what):
-            plane = xs if what == "xs" else planes[what]
-            (nc.vector if eng == "v" else nc.gpsimd).memset(plane[:].bitcast(I32), 0)
-
-        def warm():
-            seed = keep.tile([P, 2], F32, name="seed")
-            nc.vector.memset(seed[:, 0:1], 0.0)
-            nc.scalar.activation(out=seed[:, 1:2], in_=seed[:, 0:1], func=SIGMOID)
+        def load_scales(on, w, q0, q1, e0, e1):
+            rows = scales_hbm[w].rearrange("e s (q r) i -> q r (e s) i", r=4)
+            for q in range(q0, q1):
+                queue[on].dma_start(out=planes[w][32 * q : 32 * q + 4, e0:e1, :].bitcast(I32),
+                                    in_=rows[q][:, e0:e1, :].bitcast(I32))
 
         def identity():
             make_identity(nc, ident[:])
 
-        steps = {"load": load, "cast": cast, "gw": gather_words, "gb": gather_bytes, "go": gather_own, "qo": quant_own,
-                 "hid": hidden, "turn": turn, "qh": quant_h, "sf": second_far, "so": second_own, "sc": scatter, "zero": zero, "ident": identity, "warm": warm}
-        for step in PROGRAM:
-            steps[step[0]](*step[1:])
+        def load_sigmoid_table():
+            seed = keep.tile([P, 2], F32, name="seed")
+            nc.vector.memset(seed[:, 0:1], 0.0)
+            nc.scalar.activation(out=seed[:, 1:2], in_=seed[:, 0:1], func=SIGMOID)
+
+        def gathered_tile(what, j, dtype):
+            name = "far_%s%d" % (what, j)
+            tag = sigmoid_tag(*REUSES_SIGMOID_TILE[what, j]) if (what, j) in REUSES_SIGMOID_TILE else name
+            made[what, FAR, j] = keep.tile([P, GROUP], dtype, name=name, tag=tag, align_bytes=64)
+            return made[what, FAR, j]
+
+        def gather_words(j):
+            nc.vector.tensor_copy(gathered_tile("words", j, U32)[:],
+                                  far_words[:].bitcast(U32).indirect(far_list[:, list_columns(j)]))
+
+        def gather_scales(j):
+            nc.vector.tensor_copy(gathered_tile("scales", j, U8)[:], far_plane[:].indirect(far_list[:, list_columns(j)]))
+
+        def round_xo(u):
+            nc.scalar.copy(out=xo_pairs[u][:], in_=xo_raw[u][:].rearrange("p v t -> p t v"))
+
+        def gather_own(j, u):
+            if ("pairs", j) not in made:
+                made["pairs", j] = keep.tile([P, 2, 2 * GROUP], BF16, name="pairs%d" % j, align_bytes=64)
+            window = xo_pairs[u][:].rearrange("p t v -> p (t v)").bitcast(U32)
+            nc.vector.tensor_copy(made["pairs", j][:, u, :].bitcast(U32), window.indirect(own_list[:, list_columns(j)]))
+
+        def quantize(name, values):
+            codes = keep.tile([P, GROUP], U32, name=name + "_words", align_bytes=64)
+            scales = keep.tile([P, GROUP], U8, name=name + "_scales", align_bytes=64)
+            nc.vector.quantize_mx(out=codes[:].bitcast(FP8X4), scales=scales[:], in_=values[:])
+            return codes, scales
+
+        def quantize_own(j):
+            tokens = keep.tile([P, 4 * GROUP], BF16, name="own_tokens%d" % j, align_bytes=64)
+            nc.scalar.copy(out=tokens[:].bitcast(F32).rearrange("p (s u) -> p s u", u=2),
+                           in_=made["pairs", j][:].bitcast(F32).rearrange("p u s -> p s u"))
+            made["words", OWN, j], made["scales", OWN, j] = quantize("own%d" % j, tokens)
+
+        def hidden(kind, j, part):
+            expert = j if kind == FAR else 2 * j + part
+            slots = slice(part * P, (part + 1) * P)
+            w1_sums, w3_sums = next_tile("w1_sums"), next_tile("w3_sums")
+            for sums, w in ((w1_sums, "w1"), (w3_sums, "w3")):
+                nc.tensor.matmul_mx(out=sums[:], lhsT=made["words", kind, j][:, slots].bitcast(FP8X4),
+                                    lhsT_scale=made["scales", kind, j][:, slots],
+                                    rhs=words[w][:, expert, :].bitcast(FP4X4), rhs_scale=planes[w][:, expert, :],
+                                    start=True, stop=True)
+            tag = sigmoid_tag(kind, j, part)
+            sigmoid = keep.tile([P, 2, P, 2], F32, name=tag, tag=tag, align_bytes=64)
+            nc.scalar.activation(out=sigmoid[:], in_=w1_sums[:].rearrange("s (p u v) -> s u p v", u=2, v=2), func=SIGMOID)
+            h = next_tile("h")
+            nc.vector.tensor_tensor(out=h[:].rearrange("s (u p v) -> s u p v", u=2, v=2),
+                                    in0=w3_sums[:].rearrange("s (p u v) -> s u p v", u=2, v=2), in1=sigmoid[:], op=MULT)
+            made["h", kind, j, part] = h
+
+        def turn(kind, j):
+            bank = next_tile("turn_bank")
+            for part in range(2):
+                for u in range(2):
+                    nc.tensor.transpose(bank[:, part, u, :], made["h", kind, j, part][:].bitcast(F32)[:, u * P : (u + 1) * P],
+                                        ident[:])
+            turned = next_tile("turned")
+            nc.scalar.copy(out=turned[:].bitcast(F32).rearrange("p (part s u) -> p part s u", part=2, u=2),
+                           in_=bank[:].rearrange("p part u s -> p part s u"))
+            made["turned", kind, j] = turned
+
+        def quantize_hidden(kind, j):
+            made["h_mx", kind, j] = quantize("h_%s%d" % (kind, j), made["turned", kind, j])
+
+        def times_w2(sums, expert, half, kind, j, slots):
+            codes, scales = made["h_mx", kind, j]
+            nc.tensor.matmul_mx(out=sums, lhsT=words["w2"][:, expert, half * 2 * P : (half + 1) * 2 * P].bitcast(FP4X4),
+                                lhsT_scale=planes["w2"][:, expert, half * P : (half + 1) * P],
+                                rhs=codes[:, slots].bitcast(FP8X4), rhs_scale=scales[:, slots], start=True, stop=True)
+
+        def second_far(j):
+            bank = next_tile("out_bank")
+            for half in range(2):
+                times_w2(bank[:, half, :], j, half, FAR, j, slice(0, GROUP))
+            made["z", j] = keep.tile([P, 2, GROUP], F32, name="z%d" % j, align_bytes=64)
+            nc.scalar.copy(out=made["z", j][:], in_=bank[:])
+
+        def second_far_half(j, half):
+            sums = next_tile("out_bank")[:, 0, :]
+            times_w2(sums, j, half, FAR, j, slice(0, GROUP))
+            made["z", j, half] = keep.tile([P, GROUP], F32, name="z%d_%d" % (j, half))
+            nc.scalar.copy(out=made["z", j, half][:], in_=sums)
+
+        def second_own(j, half):
+            sums = next_tile("out_bank")[:, 0, :]
+            for part in range(2):
+                slots = slice(part * P, (part + 1) * P)
+                times_w2(sums[:, slots], 2 * j + part, half, OWN, j, slots)
+            made["y", j, half] = keep.tile([P, GROUP], F32, name="y%d_%d" % (j, half), align_bytes=64)
+            nc.scalar.copy(out=made["y", j, half][:], in_=sums)
+
+        def scatter(j, half):
+            nc.vector.tensor_tensor(own_out[half][:].indirect(own_list[:, list_columns(j)]), made["y", j, half][:],
+                                    gate_sb[:, j * GROUP : (j + 1) * GROUP], MULT)
+
+        def store_far(on, j):
+            queue[on].dma_start(out=out.rearrange("(half p) c -> p half c", p=P)[:, :, T + j * D : T + (j + 1) * D],
+                                in_=made["z", j][:])
+
+        def store_far_half(on, j, half):
+            queue[on].dma_start(out=out[half * P : (half + 1) * P, T + j * D : T + (j + 1) * D], in_=made["z", j, half][:])
+
+        def store_own(on, half):
+            queue[on].dma_start(out=out[half * P : (half + 1) * P, 0:T], in_=own_out[half][:])
+
+        step_by_name = {
+            "zero": zero, "load_far_list": load_far_list, "load_own_list": load_own_list, "load_x_words": load_x_words,
+            "load_x_scales": load_x_scales, "load_xo": load_xo, "load_gate": load_gate, "load_words": load_words,
+            "load_scales": load_scales, "identity": identity, "load_sigmoid_table": load_sigmoid_table,
+            "gather_words": gather_words, "gather_scales": gather_scales, "round_xo": round_xo, "gather_own": gather_own,
+            "quantize_own": quantize_own, "hidden": hidden, "turn": turn, "quantize_hidden": quantize_hidden,
+            "second_far": second_far, "second_far_half": second_far_half, "second_own": second_own, "scatter": scatter,
+            "store_far": store_far, "store_far_half": store_far_half, "store_own": store_own,
+        }
+        for step in STEPS:
+            step_by_name[step[0]](*step[1:])

from contextlib import ExitStack

import concourse.mybir as mybir
from concourse.masks import make_identity

K, T, Q, E, C, D, H, N = 512, 768, 512, 6, 128, 256, 512, 256
FLOPS = 2 * E * (C + D) * (2 * K * H + H * N)

F32 = mybir.dt.float32
BF16 = mybir.dt.bfloat16
I32 = mybir.dt.int32
U32 = mybir.dt.uint32
U16 = mybir.dt.uint16
U8 = mybir.dt.uint8
FP8X4 = mybir.dt.float8_e4m3fn_x4
FP4X4 = mybir.dt.float4_e2m1fn_x4
MULT = mybir.AluOpType.mult
SIGMOID = mybir.ActivationFunctionType.Sigmoid

P = 128
GROUP = 256
PER_COLUMN = 16
FAR, OWN = "far", "own"
SYNC, SCALAR = "sync", "scalar"

W1_BANKS, W3_BANKS, TURN_BANKS, OUT_BANKS = 2, 3, 1, 2
H_TILES = 9
TURNED_TILES = 3

REUSES_SIGMOID_TILE = {("scales", 3): (OWN, 0, 1), ("words", 3): (OWN, 1, 0), ("words", 4): (FAR, 1, 0)}

STEPS = [
    ("zero", "x"), ("zero", "w2"), ("load_far_list",), ("load_x_words", SYNC), ("zero", "w1"), ("load_x_scales", SYNC, 2, 4),
    ("load_xo", SYNC, 0), ("load_x_scales", SCALAR, 0, 2), ("load_xo", SYNC, 1), ("load_own_list",),
    ("load_words", SYNC, "w1", 0, 2), ("load_scales", SYNC, "w1", 2, 4, 0, 2), ("gather_scales", 0), ("round_xo", 1),
    ("load_scales", SCALAR, "w1", 0, 2, 0, 6), ("zero", "w3"), ("round_xo", 0), ("gather_words", 2), ("gather_own", 0, 0),
    ("load_words", SYNC, "w3", 0, 2), ("load_words", SYNC, "w1", 2, 4), ("identity",), ("load_sigmoid_table",),
    ("load_scales", SCALAR, "w3", 2, 4, 0, 2), ("load_scales", SCALAR, "w3", 0, 2, 0, 6), ("gather_scales", 1),
    ("gather_own", 2, 0), ("gather_scales", 2), ("gather_own", 1, 0), ("load_words", SYNC, "w2", 0, 2), ("gather_words", 0),
    ("gather_own", 1, 1), ("load_words", SYNC, "w1", 4, 6), ("gather_words", 1), ("gather_own", 0, 1), ("hidden", FAR, 1, 1),
    ("load_scales", SCALAR, "w1", 2, 4, 2, 6), ("hidden", FAR, 0, 0), ("quantize_own", 0), ("load_words", SYNC, "w3", 2, 4),
    ("gather_own", 2, 1), ("quantize_own", 1), ("hidden", FAR, 1, 0), ("hidden", FAR, 0, 1), ("hidden", OWN, 0, 0),
    ("gather_words", 4), ("load_scales", SYNC, "w3", 2, 4, 2, 6), ("hidden", OWN, 0, 1), ("turn", FAR, 1), ("turn", OWN, 0),
    ("load_gate", SYNC), ("quantize_own", 2), ("hidden", OWN, 1, 0), ("load_words", SYNC, "w3", 4, 6),
    ("load_scales", SYNC, "w2", 0, 2, 0, 6), ("load_scales", SYNC, "w2", 2, 4, 0, 6), ("quantize_hidden", FAR, 1),
    ("turn", FAR, 0), ("gather_words", 5), ("quantize_hidden", OWN, 0), ("hidden", OWN, 1, 1), ("hidden", FAR, 2, 1),
    ("turn", OWN, 1), ("load_words", SYNC, "w2", 2, 6), ("second_own", 0, 0), ("quantize_hidden", FAR, 0),
    ("gather_words", 3), ("quantize_hidden", OWN, 1), ("hidden", OWN, 2, 0), ("hidden", OWN, 2, 1), ("gather_scales", 3),
    ("hidden", FAR, 2, 0), ("scatter", 0, 0), ("gather_scales", 5), ("hidden", FAR, 5, 0), ("second_own", 0, 1),
    ("second_far", 0), ("gather_scales", 4), ("hidden", FAR, 3, 0), ("turn", OWN, 2), ("turn", FAR, 2),
    ("hidden", FAR, 3, 1), ("second_own", 1, 0), ("quantize_hidden", OWN, 2), ("quantize_hidden", FAR, 2),
    ("hidden", FAR, 5, 1), ("scatter", 1, 0), ("second_far", 1), ("hidden", FAR, 4, 0), ("hidden", FAR, 4, 1),
    ("turn", FAR, 3), ("second_own", 1, 1), ("store_far", SYNC, 0), ("quantize_hidden", FAR, 3), ("turn", FAR, 4),
    ("second_far", 2), ("turn", FAR, 5), ("quantize_hidden", FAR, 4), ("quantize_hidden", FAR, 5), ("second_own", 2, 0),
    ("second_far", 3), ("scatter", 0, 1), ("scatter", 1, 1), ("second_own", 2, 1), ("store_far", SCALAR, 2),
    ("second_far_half", 4, 1), ("scatter", 2, 0), ("second_far_half", 4, 0), ("second_far_half", 5, 0),
    ("store_far", SYNC, 3), ("store_far_half", SYNC, 4, 1), ("store_far", SCALAR, 1), ("scatter", 2, 1),
    ("store_far_half", SCALAR, 5, 0), ("store_far_half", SCALAR, 4, 0), ("store_own", SCALAR, 1), ("second_far_half", 5, 1),
    ("store_own", SCALAR, 0), ("store_far_half", SYNC, 5, 1),
]


def tile_moe_loc_glu_sigmoid_kernel(
    tc, x_words, x_scales, xo, w1_words, w1_scales, w3_words, w3_scales, w2_words, w2_scales, gate, offs, offs2, out
):
    nc = tc.nc
    with ExitStack() as ctx:
        keep = ctx.enter_context(tc.tile_pool(name="keep", bufs=1))
        psum = ctx.enter_context(tc.psum_pool(name="psum", bufs=1))
        queue = {SYNC: nc.sync, SCALAR: nc.scalar}

        own_list = keep.tile([P, E * C // PER_COLUMN], U16, name="own_list")
        far_list = keep.tile([P, E * D // PER_COLUMN], U16, name="far_list")
        far_words = keep.tile([P, Q], I32, name="far_words", align_bytes=64)
        far_plane = keep.tile([P, Q], U8, name="far_plane", align_bytes=64)
        width = {"w1": H, "w3": H, "w2": N}
        words = {w: keep.tile([P, E, 2 * width[w]], U8, name=w + "_words", align_bytes=64) for w in width}
        planes = {w: keep.tile([P, E, width[w]], U8, name=w + "_plane", align_bytes=64) for w in width}
        words_hbm = {"w1": w1_words, "w3": w3_words, "w2": w2_words}
        scales_hbm = {"w1": w1_scales, "w3": w3_scales, "w2": w2_scales}
        ident = keep.tile([P, P], F32, name="ident")
        gate_sb = keep.tile([P, E * C], F32, name="gate_sb")
        xo_rows = xo.rearrange("(p u v) t -> u p v t", u=2, v=2)
        xo_raw = [keep.tile([P, 2, T], F32, name="xo_raw%d" % u) for u in range(2)]
        xo_pairs = [keep.tile([P, T, 2], BF16, name="xo_pairs%d" % u) for u in range(2)]
        own_out = [keep.tile([P, T], F32, name="own_out%d" % half) for half in range(2)]

        def several(pool, name, shape, dtype, count, align):
            return [pool.tile(shape, dtype, name="%s%d" % (name, i), align_bytes=align) for i in range(count)]

        in_turn = {
            "w1_sums": several(psum, "w1_sums", [P, H], F32, W1_BANKS, None),
            "w3_sums": several(psum, "w3_sums", [P, H], F32, W3_BANKS, None),
            "turn_bank": several(psum, "turn_bank", [P, 2, 2, P], F32, TURN_BANKS, None),
            "out_bank": several(psum, "out_bank", [P, 2, GROUP], F32, OUT_BANKS, None),
            "h": several(keep, "h", [P, H], BF16, H_TILES, 64),
            "turned": several(keep, "turned", [P, 4 * GROUP], BF16, TURNED_TILES, 64),
        }
        uses = {}

        def next_tile(name):
            uses[name] = uses.get(name, -1) + 1
            return in_turn[name][uses[name] % len(in_turn[name])]

        made = {}

        def list_columns(j):
            return slice(j * GROUP // PER_COLUMN, (j + 1) * GROUP // PER_COLUMN)

        def sigmoid_tag(kind, j, part):
            return "sigmoid_%s%d%d" % (kind, j, part)

        def zero(name):
            plane = far_plane if name == "x" else planes[name]
            nc.vector.memset(plane[:].bitcast(I32), 0)

        def load_far_list():
            nc.sync.dma_start(far_list[:], offs2)

        def load_own_list():
            nc.sync.dma_start(own_list[:], offs)

        def load_x_words(on):
            queue[on].dma_start(out=far_words[:], in_=x_words[0].rearrange("p t d -> p (t d)").bitcast(I32))

        def load_x_scales(on, q0, q1):
            for q in range(q0, q1):
                queue[on].dma_start(out=far_plane[32 * q : 32 * q + 4, :].bitcast(I32),
                                    in_=x_scales[0, 4 * q : 4 * q + 4, :].bitcast(I32))

        def load_xo(on, u):
            queue[on].dma_start(out=xo_raw[u][:], in_=xo_rows[u])

        def load_gate(on):
            queue[on].dma_start(out=gate_sb[:], in_=gate)

        def load_words(on, w, e0, e1):
            queue[on].dma_start(out=words[w][:, e0:e1, :].bitcast(I32),
                                in_=words_hbm[w].rearrange("e s p b -> p (e s) b")[:, e0:e1, :].bitcast(I32))

        def load_scales(on, w, q0, q1, e0, e1):
            rows = scales_hbm[w].rearrange("e s (q r) i -> q r (e s) i", r=4)
            for q in range(q0, q1):
                queue[on].dma_start(out=planes[w][32 * q : 32 * q + 4, e0:e1, :].bitcast(I32),
                                    in_=rows[q][:, e0:e1, :].bitcast(I32))

        def identity():
            make_identity(nc, ident[:])

        def load_sigmoid_table():
            seed = keep.tile([P, 2], F32, name="seed")
            nc.vector.memset(seed[:, 0:1], 0.0)
            nc.scalar.activation(out=seed[:, 1:2], in_=seed[:, 0:1], func=SIGMOID)

        def gathered_tile(what, j, dtype):
            name = "far_%s%d" % (what, j)
            tag = sigmoid_tag(*REUSES_SIGMOID_TILE[what, j]) if (what, j) in REUSES_SIGMOID_TILE else name
            made[what, FAR, j] = keep.tile([P, GROUP], dtype, name=name, tag=tag, align_bytes=64)
            return made[what, FAR, j]

        def gather_words(j):
            nc.vector.tensor_copy(gathered_tile("words", j, U32)[:],
                                  far_words[:].bitcast(U32).indirect(far_list[:, list_columns(j)]))

        def gather_scales(j):
            nc.vector.tensor_copy(gathered_tile("scales", j, U8)[:], far_plane[:].indirect(far_list[:, list_columns(j)]))

        def round_xo(u):
            nc.scalar.copy(out=xo_pairs[u][:], in_=xo_raw[u][:].rearrange("p v t -> p t v"))

        def gather_own(j, u):
            if ("pairs", j) not in made:
                made["pairs", j] = keep.tile([P, 2, 2 * GROUP], BF16, name="pairs%d" % j, align_bytes=64)
            window = xo_pairs[u][:].rearrange("p t v -> p (t v)").bitcast(U32)
            nc.vector.tensor_copy(made["pairs", j][:, u, :].bitcast(U32), window.indirect(own_list[:, list_columns(j)]))

        def quantize(name, values):
            codes = keep.tile([P, GROUP], U32, name=name + "_words", align_bytes=64)
            scales = keep.tile([P, GROUP], U8, name=name + "_scales", align_bytes=64)
            nc.vector.quantize_mx(out=codes[:].bitcast(FP8X4), scales=scales[:], in_=values[:])
            return codes, scales

        def quantize_own(j):
            tokens = keep.tile([P, 4 * GROUP], BF16, name="own_tokens%d" % j, align_bytes=64)
            nc.scalar.copy(out=tokens[:].bitcast(F32).rearrange("p (s u) -> p s u", u=2),
                           in_=made["pairs", j][:].bitcast(F32).rearrange("p u s -> p s u"))
            made["words", OWN, j], made["scales", OWN, j] = quantize("own%d" % j, tokens)

        def hidden(kind, j, part):
            expert = j if kind == FAR else 2 * j + part
            slots = slice(part * P, (part + 1) * P)
            w1_sums, w3_sums = next_tile("w1_sums"), next_tile("w3_sums")
            for sums, w in ((w1_sums, "w1"), (w3_sums, "w3")):
                nc.tensor.matmul_mx(out=sums[:], lhsT=made["words", kind, j][:, slots].bitcast(FP8X4),
                                    lhsT_scale=made["scales", kind, j][:, slots],
                                    rhs=words[w][:, expert, :].bitcast(FP4X4), rhs_scale=planes[w][:, expert, :],
                                    start=True, stop=True)
            tag = sigmoid_tag(kind, j, part)
            sigmoid = keep.tile([P, 2, P, 2], F32, name=tag, tag=tag, align_bytes=64)
            nc.scalar.activation(out=sigmoid[:], in_=w1_sums[:].rearrange("s (p u v) -> s u p v", u=2, v=2), func=SIGMOID)
            h = next_tile("h")
            nc.vector.tensor_tensor(out=h[:].rearrange("s (u p v) -> s u p v", u=2, v=2),
                                    in0=w3_sums[:].rearrange("s (p u v) -> s u p v", u=2, v=2), in1=sigmoid[:], op=MULT)
            made["h", kind, j, part] = h

        def turn(kind, j):
            bank = next_tile("turn_bank")
            for part in range(2):
                for u in range(2):
                    nc.tensor.transpose(bank[:, part, u, :], made["h", kind, j, part][:].bitcast(F32)[:, u * P : (u + 1) * P],
                                        ident[:])
            turned = next_tile("turned")
            nc.scalar.copy(out=turned[:].bitcast(F32).rearrange("p (part s u) -> p part s u", part=2, u=2),
                           in_=bank[:].rearrange("p part u s -> p part s u"))
            made["turned", kind, j] = turned

        def quantize_hidden(kind, j):
            made["h_mx", kind, j] = quantize("h_%s%d" % (kind, j), made["turned", kind, j])

        def times_w2(sums, expert, half, kind, j, slots):
            codes, scales = made["h_mx", kind, j]
            nc.tensor.matmul_mx(out=sums, lhsT=words["w2"][:, expert, half * 2 * P : (half + 1) * 2 * P].bitcast(FP4X4),
                                lhsT_scale=planes["w2"][:, expert, half * P : (half + 1) * P],
                                rhs=codes[:, slots].bitcast(FP8X4), rhs_scale=scales[:, slots], start=True, stop=True)

        def second_far(j):
            bank = next_tile("out_bank")
            for half in range(2):
                times_w2(bank[:, half, :], j, half, FAR, j, slice(0, GROUP))
            made["z", j] = keep.tile([P, 2, GROUP], F32, name="z%d" % j, align_bytes=64)
            nc.scalar.copy(out=made["z", j][:], in_=bank[:])

        def second_far_half(j, half):
            sums = next_tile("out_bank")[:, 0, :]
            times_w2(sums, j, half, FAR, j, slice(0, GROUP))
            made["z", j, half] = keep.tile([P, GROUP], F32, name="z%d_%d" % (j, half))
            nc.scalar.copy(out=made["z", j, half][:], in_=sums)

        def second_own(j, half):
            sums = next_tile("out_bank")[:, 0, :]
            for part in range(2):
                slots = slice(part * P, (part + 1) * P)
                times_w2(sums[:, slots], 2 * j + part, half, OWN, j, slots)
            made["y", j, half] = keep.tile([P, GROUP], F32, name="y%d_%d" % (j, half), align_bytes=64)
            nc.scalar.copy(out=made["y", j, half][:], in_=sums)

        def scatter(j, half):
            nc.vector.tensor_tensor(own_out[half][:].indirect(own_list[:, list_columns(j)]), made["y", j, half][:],
                                    gate_sb[:, j * GROUP : (j + 1) * GROUP], MULT)

        def store_far(on, j):
            queue[on].dma_start(out=out.rearrange("(half p) c -> p half c", p=P)[:, :, T + j * D : T + (j + 1) * D],
                                in_=made["z", j][:])

        def store_far_half(on, j, half):
            queue[on].dma_start(out=out[half * P : (half + 1) * P, T + j * D : T + (j + 1) * D], in_=made["z", j, half][:])

        def store_own(on, half):
            queue[on].dma_start(out=out[half * P : (half + 1) * P, 0:T], in_=own_out[half][:])

        step_by_name = {
            "zero": zero, "load_far_list": load_far_list, "load_own_list": load_own_list, "load_x_words": load_x_words,
            "load_x_scales": load_x_scales, "load_xo": load_xo, "load_gate": load_gate, "load_words": load_words,
            "load_scales": load_scales, "identity": identity, "load_sigmoid_table": load_sigmoid_table,
            "gather_words": gather_words, "gather_scales": gather_scales, "round_xo": round_xo, "gather_own": gather_own,
            "quantize_own": quantize_own, "hidden": hidden, "turn": turn, "quantize_hidden": quantize_hidden,
            "second_far": second_far, "second_far_half": second_far_half, "second_own": second_own, "scatter": scatter,
            "store_far": store_far, "store_far_half": store_far_half, "store_own": store_own,
        }
        for step in STEPS:
            step_by_name[step[0]](*step[1:])
